import numpy as np
import ml_dtypes


def mxq(x, axis, fmt="e4m3"):
    dtype, down = {"e4m3": (ml_dtypes.float8_e4m3fn, 7), "e5m2": (ml_dtypes.float8_e5m2, 14)}[fmt]
    v = np.moveaxis(np.asarray(x, np.float32).astype(ml_dtypes.bfloat16).astype(np.float64), axis, -1)
    blocks = v.reshape(v.shape[:-1] + (-1, 32))
    amax = np.abs(blocks).max(-1, keepdims=True)
    byte = np.maximum(np.where(amax > 0, np.frexp(amax)[1] - 1 + 127, 0) - down, 1)
    scale = np.exp2(byte - 127.0)
    codes = (blocks / scale).astype(np.float32).astype(dtype).astype(np.float64)
    return np.moveaxis((codes * scale).reshape(v.shape), -1, axis)


WIDE = False


def mx_kscale(k):
    if not WIDE:
        return np.ones(k)
    levels = np.array([10, -10, 5, -5, 0])
    if k % 512:
        return np.exp2(np.random.permutation(np.resize(levels, k // 32))).repeat(32)
    a = np.empty((k // 512, 16))
    for p in range(k // 512):
        a[p, :8] = np.random.permutation(np.resize(levels, 8))
        for g in range(8):
            far = levels[np.abs(levels - a[p, g]) >= 10]
            a[p, g + 8] = far[np.random.randint(len(far))]
    return np.exp2(a.ravel()).repeat(32)


BF16 = ml_dtypes.bfloat16


def bf(x):
    return np.asarray(x, np.float32).astype(BF16)


def f64(x):
    return np.asarray(x).astype(np.float64)


E2M1 = np.array([0.0, 0.5, 1.0, 1.5, 2.0, 3.0, 4.0, 6.0, -0.0, -0.5, -1.0, -1.5, -2.0, -3.0, -4.0, -6.0])


def pack_weight(w, fmt):
    k, n = w.shape
    w = f64(bf(w)).reshape(k // 32, 32, n)
    amax = np.abs(w).max(1)
    if fmt == "e4m3":
        byte = np.frexp(amax)[1] - 1 + 127 - 7
    else:
        mant, ex = np.frexp(amax / 6.0)
        byte = np.where(mant > 0.5, ex, ex - 1) + 127
    byte = np.clip(np.where(amax > 0, byte, 1), 1, 254)
    scaled = (w * np.exp2(127.0 - byte)[:, None, :]).reshape(k, n).astype(np.float32)
    by_word = np.ascontiguousarray(scaled.reshape(k // 512, 128, 4, n).transpose(0, 1, 3, 2))
    if fmt == "e4m3":
        words = by_word.astype(ml_dtypes.float8_e4m3fn).view(np.uint8)
    else:
        c = by_word.astype(ml_dtypes.float4_e2m1fn).view(np.uint8) & 0xF
        words = c[..., 0::2] | (c[..., 1::2] << 4)
    return np.ascontiguousarray(words), np.ascontiguousarray(byte.astype(np.uint8).reshape(k // 512, 16, n))


def unpack_weight(words, scales, fmt):
    g, p, n, _ = words.shape
    if fmt == "e4m3":
        vals = np.ascontiguousarray(words).view(ml_dtypes.float8_e4m3fn).astype(np.float64)
    else:
        nib = np.empty((g, p, n, 4), np.uint8)
        nib[..., 0::2] = words & 0xF
        nib[..., 1::2] = words >> 4
        vals = E2M1[nib]
    vals = vals * np.repeat(np.exp2(scales.astype(np.float64) - 127.0), 8, axis=1)[..., None]
    return vals.transpose(0, 1, 3, 2).reshape(g * 512, n)
def pack4(w):
    words, scales = pack_weight(w, "e2m1")
    return words.reshape(words.shape[0], 128, -1), scales


def unpack4(words, scales):
    return unpack_weight(words.reshape(words.shape[0], 128, -1, 2), scales, "e2m1")


def planes(Y):
    n, m = Y.shape
    b = f64(bf(Y)).reshape(n // 32, 32, m)
    amax = np.abs(b).max(1)
    byte = np.clip(np.where(amax > 0, np.frexp(amax)[1] - 1 + 127 - 7, 1), 1, 254)
    codes = (b * np.exp2(127.0 - byte)[:, None, :]).reshape(n, m).astype(np.float32).astype(ml_dtypes.float8_e4m3fn).view(np.uint8)
    words = codes.reshape(n // 512, 128, 4, m).transpose(0, 1, 3, 2)
    return np.ascontiguousarray(words), np.ascontiguousarray(byte.astype(np.uint8).reshape(n // 512, 16, m))


B, S, D, R = 4, 512, 2560, 1024

BIAS_SIZE = 0.3
GAIN_SPREAD = 0.8


def setup_inputs():
    s = mx_kscale(D)
    hidden = np.random.randn(B, S, D) / s
    w = np.random.randn(D, R) / np.sqrt(D)
    w_words, w_scales = pack4(w * s[:, None])
    bias = BIAS_SIZE * np.random.randn(R)
    gain = np.exp(GAIN_SPREAD * np.random.randn(R))
    return {"hidden": bf(hidden), "w_words": w_words, "w_scales": w_scales,
            "bias": bf(bias), "gain": bf(gain)}


def reference(hidden, w_words, w_scales, bias, gain):
    h = mxq(f64(hidden).reshape(B * S, D), 1, "e4m3")
    w = unpack4(w_words, w_scales)
    c = h @ w
    y = ((c + f64(bias)) * f64(gain)).reshape(B, S, R)
    Y = y.reshape(B * S, R).T
    words, scales = planes(Y)
    return y, words, scales

@@ -1,0 +1,273 @@
+from contextlib import ExitStack
+
+import concourse.mybir as mybir
+from concourse.masks import make_identity
+
+TOKENS, D, R = 2048, 2560, 1024
+FLOPS = 2 * TOKENS * D * R
+
+F32 = mybir.dt.float32
+BF16 = mybir.dt.bfloat16
+I32 = mybir.dt.int32
+U32 = mybir.dt.uint32
+U8 = mybir.dt.uint8
+FP8X4 = mybir.dt.float8_e4m3fn_x4
+FP4X4 = mybir.dt.float4_e2m1fn_x4
+ADD = mybir.AluOpType.add
+MULT = mybir.AluOpType.mult
+
+P = 128
+GROUP = 512
+TILES = TOKENS // P
+PASSES = D // GROUP
+HALVES = R // GROUP
+BANKS = 8
+VECTOR_PASSES = 3
+PARTS = ((0, VECTOR_PASSES), (VECTOR_PASSES, PASSES))
+BANK_PASSES = ((0, 1), (2, 3), (4,))
+CODE_CHUNKS = ((0, 4), (4, 8), (8, 12), (12, 15), (15, 16))
+SCALE_CHUNKS = ((0, 15), (15, 16))
+
+
+def tile_shared_kv_latent_gain_g4_kernel(tc, hidden, w_words, w_scales, bias, gain, out_0, out_1, out_2):
+    nc = tc.nc
+    h_rows = hidden.rearrange("b s d -> (b s) d")
+    y_rows = out_0.rearrange("b s r -> (b s) r")
+    code_rows = out_1.rearrange("g p m t -> p g (m t)")
+    w_scale_rows = w_scales.rearrange("g (q r) n -> r q g n", r=4)
+    y_scale_rows = out_2.rearrange("g (q r) m -> r q g m", r=4)
+
+    with ExitStack() as ctx:
+        keep = ctx.enter_context(tc.tile_pool(name="keep", bufs=1))
+        work = ctx.enter_context(tc.tile_pool(name="work", bufs=3))
+        psum = ctx.enter_context(tc.psum_pool(name="psum", bufs=1))
+        ctx.enter_context(tc.manual_schedule())
+
+        banks_taken = []
+
+        def take_bank():
+            tag = "bank%d" % (len(banks_taken) % BANKS)
+            banks_taken.append(tag)
+            return psum.tile([P, GROUP], F32, name=tag, tag=tag)
+
+        raw = {}
+        sorted_h = {}
+        grouped_h = {}
+        h_codes = {}
+        h_scales = {}
+        acc = {}
+        biased = {}
+        y_f32 = {}
+        y_pairs = {}
+        grouped_y = {}
+
+        ident = keep.tile([P, P], F32, name="ident")
+        w_tiles = [keep.tile([P, PASSES, 2 * GROUP], U8, name="w%d" % h, align_bytes=256) for h in range(HALVES)]
+        w_planes = [keep.tile([P, PASSES, GROUP], U8, name="wscale%d" % h, align_bytes=256) for h in range(HALVES)]
+        y_codes = [keep.tile([P, HALVES, (b - a) * P], U32, name="ycodes%d" % a, align_bytes=256) for a, b in CODE_CHUNKS]
+        y_planes = [keep.tile([P, HALVES, (b - a) * P], U8, name="yscale%d" % a, align_bytes=256) for a, b in SCALE_CHUNKS]
+        short = [keep.tile([P, R // P], BF16, name="short%d" % v) for v in range(2)]
+        spread = [keep.tile([P, R], BF16, name="spread%d" % v) for v in range(2)]
+
+        def load_h(i):
+            for part, (a, b) in enumerate(PARTS):
+                name = "raw%d_%d" % (i, part)
+                raw[i, part] = keep.tile([P, (b - a) * GROUP], BF16, name=name)
+                nc.sync.dma_start(out=raw[i, part][:], in_=h_rows[i * P : (i + 1) * P, a * GROUP : b * GROUP])
+
+        def load_w_scales(h):
+            for r in range(4):
+                nc.sync.dma_start(
+                    out=w_planes[h][r:P:32, :, :].bitcast(I32),
+                    in_=w_scale_rows[r][:, :, h * GROUP : (h + 1) * GROUP].bitcast(I32),
+                )
+
+        def load_w(h, a, b):
+            nc.sync.dma_start(
+                out=w_tiles[h][:, a:b, :].bitcast(I32),
+                in_=w_words[a:b, :, 2 * h * GROUP : 2 * (h + 1) * GROUP].rearrange("g p n -> p g n").bitcast(I32),
+            )
+
+        def sort_h(i, part):
+            a, b = PARTS[part]
+            tag = "sorted%d" % part
+            sorted_h[i, part] = work.tile([P, 2, (b - a) * P], F32, name=tag, tag=tag)
+            words = raw[i, part][:].bitcast(F32).rearrange("m (w u) -> m u w", u=2)
+            if part == 0:
+                nc.vector.tensor_copy(out=sorted_h[i, part][:], in_=words)
+            else:
+                nc.scalar.copy(out=sorted_h[i, part][:], in_=words)
+
+        def transpose_h(i):
+            for c, passes in enumerate(BANK_PASSES):
+                bank = take_bank()
+                for j, g in enumerate(passes):
+                    part = 0 if g < VECTOR_PASSES else 1
+                    local = g - PARTS[part][0]
+                    for u in range(2):
+                        col = (2 * j + u) * P
+                        nc.tensor.transpose(
+                            bank[:, col : col + P], sorted_h[i, part][:, u, local * P : (local + 1) * P], ident[:]
+                        )
+                n = len(passes)
+                tag = "grouped%d" % c
+                grouped_h[i, c] = work.tile([P, n * GROUP], BF16, name=tag, tag=tag, align_bytes=256)
+                nc.scalar.copy(
+                    out=grouped_h[i, c][:].bitcast(F32).rearrange("p (j m u) -> p j m u", j=n, u=2),
+                    in_=bank[:, : 2 * n * P].rearrange("p (j u m) -> p j m u", j=n, u=2),
+                )
+
+        def quantize_h(i):
+            for c, passes in enumerate(BANK_PASSES):
+                n = len(passes)
+                codes = work.tile([P, n * P], U32, name="hcodes%d" % c, tag="hcodes%d" % c, align_bytes=256)
+                plane = work.tile([P, n * P], U8, name="hscale%d" % c, tag="hscale%d" % c, align_bytes=256)
+                nc.vector.quantize_mx(out=codes[:].bitcast(FP8X4), scales=plane[:], in_=grouped_h[i, c][:])
+                for j, g in enumerate(passes):
+                    h_codes[i, g] = codes[:, j * P : (j + 1) * P]
+                    h_scales[i, g] = plane[:, j * P : (j + 1) * P]
+
+        def multiply(i, h):
+            acc[i, h] = take_bank()
+            for g in range(PASSES):
+                nc.tensor.matmul_mx(
+                    out=acc[i, h][:],
+                    lhsT=h_codes[i, g].bitcast(FP8X4),
+                    lhsT_scale=h_scales[i, g],
+                    rhs=w_tiles[h][:, g, :].bitcast(FP4X4),
+                    rhs_scale=w_planes[h][:, g, :],
+                    start=(g == 0),
+                    stop=(g == PASSES - 1),
+                )
+
+        def add_bias(i, h):
+            if h == 0:
+                biased[i] = work.tile([P, R], F32, name="biased", tag="biased")
+            cols = slice(h * GROUP, (h + 1) * GROUP)
+            nc.vector.tensor_tensor(out=biased[i][:, cols], in0=acc[i, h][:], in1=spread[0][:, cols], op=ADD)
+
+        def apply_gain(i, a, b):
+            if a == 0:
+                y_f32[i] = work.tile([P, R], F32, name="y", tag="y", bufs=8)
+            cols = slice(a * GROUP, b * GROUP)
+            nc.vector.tensor_tensor(out=y_f32[i][:, cols], in0=biased[i][:, cols], in1=spread[1][:, cols], op=MULT)
+            nc.sync.dma_start(out=y_rows[i * P : (i + 1) * P, cols], in_=y_f32[i][:, cols])
+
+        def round_y(i, a, b):
+            tile = work.tile([P, 2, (b - a) * P, 2], BF16, name="pairs", tag="pairs")
+            nc.scalar.copy(
+                out=tile[:], in_=y_f32[i][:, a * GROUP : b * GROUP].rearrange("m (w u e) -> m u w e", u=2, e=2)
+            )
+            words = tile[:].rearrange("m u w e -> m (u w e)").bitcast(F32).rearrange("m (u w) -> m u w", u=2)
+            for h in range(a, b):
+                y_pairs[i, h] = words[:, :, (h - a) * P : (h - a + 1) * P]
+
+        def transpose_y(i, a, b):
+            bank = take_bank()
+            n = b - a
+            for j in range(n):
+                for u in range(2):
+                    col = (2 * j + u) * P
+                    nc.tensor.transpose(bank[:, col : col + P], y_pairs[i, a + j][:, u, :], ident[:])
+            tile = work.tile([P, n * GROUP], BF16, name="groupedy", tag="groupedy", align_bytes=256)
+            nc.scalar.copy(
+                out=tile[:].bitcast(F32).rearrange("p (j m u) -> p j m u", j=n, u=2),
+                in_=bank[:, : 2 * n * P].rearrange("p (j u m) -> p j m u", j=n, u=2),
+            )
+            for j in range(n):
+                grouped_y[i, a + j] = tile[:, j * GROUP : (j + 1) * GROUP]
+
+        def quantize_y(i, a, b):
+            cc = [c for c, (lo, hi) in enumerate(CODE_CHUNKS) if lo <= i < hi][0]
+            sc = [c for c, (lo, hi) in enumerate(SCALE_CHUNKS) if lo <= i < hi][0]
+            c0 = (i - CODE_CHUNKS[cc][0]) * P
+            s0 = (i - SCALE_CHUNKS[sc][0]) * P
+            for h in range(a, b):
+                nc.vector.quantize_mx(
+                    out=y_codes[cc][:, h, c0 : c0 + P].bitcast(FP8X4),
+                    scales=y_planes[sc][:, h, s0 : s0 + P],
+                    in_=grouped_y[i, h],
+                )
+            if b == HALVES and i + 1 == CODE_CHUNKS[cc][1]:
+                lo, hi = CODE_CHUNKS[cc]
+                nc.sync.dma_start(out=code_rows[:, :, 4 * lo * P : 4 * hi * P].bitcast(I32), in_=y_codes[cc][:].bitcast(I32))
+            if b == HALVES and i + 1 == SCALE_CHUNKS[sc][1]:
+                lo, hi = SCALE_CHUNKS[sc]
+                for r in range(4):
+                    queue = nc.sync if r % 2 == 0 or hi < TILES else nc.scalar
+                    queue.dma_start(
+                        out=y_scale_rows[r][:, :, lo * P : hi * P].bitcast(I32), in_=y_planes[sc][r:P:32, :, :].bitcast(I32)
+                    )
+
+        def spread_vectors():
+            for v in range(2):
+                bank = take_bank()
+                words = short[v][:].bitcast(F32)
+                for j in range(4):
+                    nc.tensor.transpose(bank[:, j * P : (j + 1) * P], words[:, j : j + 1].to_broadcast([P, P]), ident[:])
+                nc.scalar.copy(
+                    out=spread[v][:].bitcast(F32).rearrange("m (n j) -> m n j", j=4),
+                    in_=bank[:].rearrange("m (j n) -> m n j", j=4),
+                )
+
+        for h in range(HALVES):
+            nc.vector.memset(w_planes[h][:].bitcast(I32), 0)
+        make_identity(nc, ident[:])
+        nc.gpsimd.dma_start(out=short[0][:], in_=bias.rearrange("(n c) -> n c", n=P))
+        nc.gpsimd.dma_start(out=short[1][:], in_=gain.rearrange("(n c) -> n c", n=P))
+        load_h(0)
+        load_w_scales(0)
+        load_w(0, 0, 2)
+        load_w(0, 2, PASSES)
+        load_h(1)
+        load_w_scales(1)
+        load_w(1, 0, PASSES)
+        for i in range(2, TILES):
+            load_h(i)
+
+        sort_h(0, 0)
+        sort_h(0, 1)
+        transpose_h(0)
+        quantize_h(0)
+        spread_vectors()
+        sort_h(1, 0)
+        sort_h(1, 1)
+        multiply(0, 0)
+        transpose_h(1)
+        quantize_h(1)
+        add_bias(0, 0)
+        sort_h(2, 0)
+        sort_h(2, 1)
+        multiply(0, 1)
+
+        for i in range(1, TILES):
+            if i + 1 < TILES:
+                transpose_h(i + 1)
+            if i >= 2:
+                transpose_y(i - 2, 0, HALVES)
+            add_bias(i - 1, 1)
+            if i + 2 < TILES:
+                sort_h(i + 2, 0)
+                sort_h(i + 2, 1)
+            apply_gain(i - 1, 0, HALVES)
+            round_y(i - 1, 0, HALVES)
+            if i + 1 < TILES:
+                quantize_h(i + 1)
+            if i >= 2:
+                quantize_y(i - 2, 0, HALVES)
+            multiply(i, 0)
+            add_bias(i, 0)
+            multiply(i, 1)
+
+        last = TILES - 1
+        apply_gain(last, 0, 1)
+        round_y(last, 0, 1)
+        transpose_y(last - 1, 0, HALVES)
+        transpose_y(last, 0, 1)
+        add_bias(last, 1)
+        quantize_y(last - 1, 0, HALVES)
+        apply_gain(last, 1, HALVES)
+        round_y(last, 1, HALVES)
+        quantize_y(last, 0, 1)
+        transpose_y(last, 1, HALVES)
+        quantize_y(last, 1, HALVES)

@@ -23,10 +23,9 @@ PASSES = D // GROUP
 HALVES = R // GROUP
 BANKS = 8
 VECTOR_PASSES = 3
-PARTS = ((0, VECTOR_PASSES), (VECTOR_PASSES, PASSES))
-BANK_PASSES = ((0, 1), (2, 3), (4,))
-CODE_CHUNKS = ((0, 4), (4, 8), (8, 12), (12, 15), (15, 16))
-SCALE_CHUNKS = ((0, 15), (15, 16))
+BANK_PASSES = ((0, 2), (2, 4), (4, 5))
+CODE_CHUNKS = ((0, 4), (4, 8), (8, 12), (12, 14), (14, 15), (15, 16))
+SCALE_CHUNKS = ((0, 13), (13, 16))
 
 
 def tile_shared_kv_latent_gain_g4_kernel(tc, hidden, w_words, w_scales, bias, gain, out_0, out_1, out_2):
@@ -60,6 +59,7 @@ def tile_shared_kv_latent_gain_g4_kernel(tc, hidden, w_words, w_scales, bias, ga
         y_f32 = {}
         y_pairs = {}
         grouped_y = {}
+        spread_bank = {}
 
         ident = keep.tile([P, P], F32, name="ident")
         w_tiles = [keep.tile([P, PASSES, 2 * GROUP], U8, name="w%d" % h, align_bytes=256) for h in range(HALVES)]
@@ -69,11 +69,10 @@ def tile_shared_kv_latent_gain_g4_kernel(tc, hidden, w_words, w_scales, bias, ga
         short = [keep.tile([P, R // P], BF16, name="short%d" % v) for v in range(2)]
         spread = [keep.tile([P, R], BF16, name="spread%d" % v) for v in range(2)]
 
-        def load_h(i):
-            for part, (a, b) in enumerate(PARTS):
-                name = "raw%d_%d" % (i, part)
-                raw[i, part] = keep.tile([P, (b - a) * GROUP], BF16, name=name)
-                nc.sync.dma_start(out=raw[i, part][:], in_=h_rows[i * P : (i + 1) * P, a * GROUP : b * GROUP])
+        def load_h(i, a, b):
+            tile = keep.tile([P, (b - a) * GROUP], BF16, name="raw%d_%d" % (i, a))
+            nc.sync.dma_start(out=tile[:], in_=h_rows[i * P : (i + 1) * P, a * GROUP : b * GROUP])
+            raw[i, a] = tile
 
         def load_w_scales(h):
             for r in range(4):
@@ -88,48 +87,49 @@ def tile_shared_kv_latent_gain_g4_kernel(tc, hidden, w_words, w_scales, bias, ga
                 in_=w_words[a:b, :, 2 * h * GROUP : 2 * (h + 1) * GROUP].rearrange("g p n -> p g n").bitcast(I32),
             )
 
-        def sort_h(i, part):
-            a, b = PARTS[part]
-            tag = "sorted%d" % part
-            sorted_h[i, part] = work.tile([P, 2, (b - a) * P], F32, name=tag, tag=tag)
-            words = raw[i, part][:].bitcast(F32).rearrange("m (w u) -> m u w", u=2)
-            if part == 0:
-                nc.vector.tensor_copy(out=sorted_h[i, part][:], in_=words)
+        def sort_h(i, a, b, on_vector):
+            tag = "sorted_v" if on_vector else "sorted_s"
+            tile = work.tile([P, 2, (b - a) * P], F32, name=tag, tag=tag)
+            words = raw[i, a][:].bitcast(F32).rearrange("m (w u) -> m u w", u=2)
+            if on_vector:
+                nc.vector.tensor_copy(out=tile[:], in_=words)
             else:
-                nc.scalar.copy(out=sorted_h[i, part][:], in_=words)
+                nc.scalar.copy(out=tile[:], in_=words)
+            for g in range(a, b):
+                sorted_h[i, g] = tile[:, :, (g - a) * P : (g - a + 1) * P]
 
-        def transpose_h(i):
-            for c, passes in enumerate(BANK_PASSES):
-                bank = take_bank()
-                for j, g in enumerate(passes):
-                    part = 0 if g < VECTOR_PASSES else 1
-                    local = g - PARTS[part][0]
-                    for u in range(2):
-                        col = (2 * j + u) * P
-                        nc.tensor.transpose(
-                            bank[:, col : col + P], sorted_h[i, part][:, u, local * P : (local + 1) * P], ident[:]
-                        )
-                n = len(passes)
-                tag = "grouped%d" % c
-                grouped_h[i, c] = work.tile([P, n * GROUP], BF16, name=tag, tag=tag, align_bytes=256)
-                nc.scalar.copy(
-                    out=grouped_h[i, c][:].bitcast(F32).rearrange("p (j m u) -> p j m u", j=n, u=2),
-                    in_=bank[:, : 2 * n * P].rearrange("p (j u m) -> p j m u", j=n, u=2),
-                )
+        def view_h(i, a, b):
+            words = raw[i, a][:].bitcast(F32).rearrange("m (w u) -> m u w", u=2)
+            for g in range(a, b):
+                sorted_h[i, g] = words[:, :, (g - a) * P : (g - a + 1) * P]
 
-        def quantize_h(i):
-            for c, passes in enumerate(BANK_PASSES):
-                n = len(passes)
-                codes = work.tile([P, n * P], U32, name="hcodes%d" % c, tag="hcodes%d" % c, align_bytes=256)
-                plane = work.tile([P, n * P], U8, name="hscale%d" % c, tag="hscale%d" % c, align_bytes=256)
-                nc.vector.quantize_mx(out=codes[:].bitcast(FP8X4), scales=plane[:], in_=grouped_h[i, c][:])
-                for j, g in enumerate(passes):
-                    h_codes[i, g] = codes[:, j * P : (j + 1) * P]
-                    h_scales[i, g] = plane[:, j * P : (j + 1) * P]
+        def transpose_h(i, a, b):
+            bank = take_bank()
+            n = b - a
+            for j in range(n):
+                for u in range(2):
+                    col = (2 * j + u) * P
+                    nc.tensor.transpose(bank[:, col : col + P], sorted_h[i, a + j][:, u, :], ident[:])
+            tile = work.tile([P, n * GROUP], BF16, name="grouped", tag="grouped", bufs=6, align_bytes=256)
+            nc.scalar.copy(
+                out=tile[:].bitcast(F32).rearrange("p (j m u) -> p j m u", j=n, u=2),
+                in_=bank[:, : 2 * n * P].rearrange("p (j u m) -> p j m u", j=n, u=2),
+            )
+            grouped_h[i, a] = tile
 
-        def multiply(i, h):
-            acc[i, h] = take_bank()
-            for g in range(PASSES):
+        def quantize_h(i, a, b):
+            n = b - a
+            codes = work.tile([P, n * P], U32, name="hcodes", tag="hcodes", bufs=9, align_bytes=256)
+            plane = work.tile([P, n * P], U8, name="hscale", tag="hscale", bufs=9, align_bytes=256)
+            nc.vector.quantize_mx(out=codes[:].bitcast(FP8X4), scales=plane[:], in_=grouped_h[i, a][:])
+            for j in range(n):
+                h_codes[i, a + j] = codes[:, j * P : (j + 1) * P]
+                h_scales[i, a + j] = plane[:, j * P : (j + 1) * P]
+
+        def multiply(i, h, a=0, b=PASSES):
+            if a == 0:
+                acc[i, h] = take_bank()
+            for g in range(a, b):
                 nc.tensor.matmul_mx(
                     out=acc[i, h][:],
                     lhsT=h_codes[i, g].bitcast(FP8X4),
@@ -161,6 +161,17 @@ def tile_shared_kv_latent_gain_g4_kernel(tc, hidden, w_words, w_scales, bias, ga
             words = tile[:].rearrange("m u w e -> m (u w e)").bitcast(F32).rearrange("m (u w) -> m u w", u=2)
             for h in range(a, b):
                 y_pairs[i, h] = words[:, :, (h - a) * P : (h - a + 1) * P]
+
+        def gain_and_round(i, h):
+            cols = slice(h * GROUP, (h + 1) * GROUP)
+            tile = work.tile([P, 2, P, 2], BF16, name="pairs", tag="pairs")
+            nc.vector.tensor_tensor(
+                out=tile[:],
+                in0=biased[i][:, cols].rearrange("m (w u e) -> m u w e", u=2, e=2),
+                in1=spread[1][:, cols].rearrange("m (w u e) -> m u w e", u=2, e=2),
+                op=MULT,
+            )
+            y_pairs[i, h] = tile[:].rearrange("m u w e -> m (u w e)").bitcast(F32).rearrange("m (u w) -> m u w", u=2)
 
         def transpose_y(i, a, b):
             bank = take_bank()
@@ -199,75 +210,141 @@ def tile_shared_kv_latent_gain_g4_kernel(tc, hidden, w_words, w_scales, bias, ga
                         out=y_scale_rows[r][:, :, lo * P : hi * P].bitcast(I32), in_=y_planes[sc][r:P:32, :, :].bitcast(I32)
                     )
 
-        def spread_vectors():
-            for v in range(2):
-                bank = take_bank()
-                words = short[v][:].bitcast(F32)
-                for j in range(4):
-                    nc.tensor.transpose(bank[:, j * P : (j + 1) * P], words[:, j : j + 1].to_broadcast([P, P]), ident[:])
-                nc.scalar.copy(
-                    out=spread[v][:].bitcast(F32).rearrange("m (n j) -> m n j", j=4),
-                    in_=bank[:].rearrange("m (j n) -> m n j", j=4),
+        def spread_transpose(v):
+            spread_bank[v] = take_bank()
+            words = short[v][:].bitcast(F32)
+            for j in range(4):
+                nc.tensor.transpose(
+                    spread_bank[v][:, j * P : (j + 1) * P], words[:, j : j + 1].to_broadcast([P, P]), ident[:]
                 )
 
+        def spread_copy(v):
+            nc.scalar.copy(
+                out=spread[v][:].bitcast(F32).rearrange("m (n j) -> m n j", j=4),
+                in_=spread_bank[v][:].rearrange("m (j n) -> m n j", j=4),
+            )
+
+        def finish_in_quarters(i, h):
+            pairs = work.tile([P, 2, P, 2], BF16, name="pairs", tag="pairs")
+            quarter_cols = [slice(h * GROUP + q * P, h * GROUP + (q + 1) * P) for q in range(4)]
+
+            def quarter_pairs(q):
+                nc.vector.tensor_tensor(
+                    out=pairs[:, :, q * 32 : (q + 1) * 32, :],
+                    in0=biased[i][:, quarter_cols[q]].rearrange("m (w u e) -> m u w e", u=2, e=2),
+                    in1=spread[1][:, quarter_cols[q]].rearrange("m (w u e) -> m u w e", u=2, e=2),
+                    op=MULT,
+                )
+
+            for q in range(4):
+                bank = take_bank()
+                for g in range(PASSES):
+                    nc.tensor.matmul_mx(
+                        out=bank[:, :P],
+                        lhsT=h_codes[i, g].bitcast(FP8X4),
+                        lhsT_scale=h_scales[i, g],
+                        rhs=w_tiles[h][:, g, 2 * q * P : 2 * (q + 1) * P].bitcast(FP4X4),
+                        rhs_scale=w_planes[h][:, g, q * P : (q + 1) * P],
+                        start=(g == 0),
+                        stop=(g == PASSES - 1),
+                    )
+                nc.vector.tensor_tensor(
+                    out=biased[i][:, quarter_cols[q]], in0=bank[:, :P], in1=spread[0][:, quarter_cols[q]], op=ADD
+                )
+                if q > 0:
+                    quarter_pairs(q - 1)
+            quarter_pairs(3)
+            y_pairs[i, h] = pairs[:].rearrange("m u w e -> m (u w e)").bitcast(F32).rearrange("m (u w) -> m u w", u=2)
+
+        nc.scalar.dma_start(out=short[0][:], in_=bias.rearrange("(n c) -> n c", n=P))
+        nc.scalar.dma_start(out=short[1][:], in_=gain.rearrange("(n c) -> n c", n=P))
         for h in range(HALVES):
             nc.vector.memset(w_planes[h][:].bitcast(I32), 0)
         make_identity(nc, ident[:])
-        nc.gpsimd.dma_start(out=short[0][:], in_=bias.rearrange("(n c) -> n c", n=P))
-        nc.gpsimd.dma_start(out=short[1][:], in_=gain.rearrange("(n c) -> n c", n=P))
-        load_h(0)
+        for a, b in BANK_PASSES:
+            load_h(0, a, b)
         load_w_scales(0)
         load_w(0, 0, 2)
         load_w(0, 2, PASSES)
-        load_h(1)
+        load_h(1, 0, VECTOR_PASSES)
+        load_h(1, VECTOR_PASSES, PASSES)
         load_w_scales(1)
-        load_w(1, 0, PASSES)
+        load_w(1, 0, 2)
+        load_w(1, 2, PASSES)
         for i in range(2, TILES):
-            load_h(i)
+            load_h(i, 0, VECTOR_PASSES)
+            load_h(i, VECTOR_PASSES, PASSES)
 
-        sort_h(0, 0)
-        sort_h(0, 1)
-        transpose_h(0)
-        quantize_h(0)
-        spread_vectors()
-        sort_h(1, 0)
-        sort_h(1, 1)
+        def sort_tile(i):
+            sort_h(i, 0, VECTOR_PASSES, True)
+            sort_h(i, VECTOR_PASSES, PASSES, False)
+
+        def transpose_tile(i):
+            for a, b in BANK_PASSES:
+                transpose_h(i, a, b)
+
+        def quantize_tile(i):
+            for a, b in BANK_PASSES:
+                quantize_h(i, a, b)
+
+        for a, b in BANK_PASSES:
+            sort_h(0, a, b, True)
+        spread_transpose(0)
+        transpose_tile(0)
+        spread_transpose(1)
+        spread_copy(0)
+        spread_copy(1)
+        quantize_tile(0)
+        sort_tile(1)
         multiply(0, 0)
-        transpose_h(1)
-        quantize_h(1)
+        transpose_tile(1)
         add_bias(0, 0)
-        sort_h(2, 0)
-        sort_h(2, 1)
+        quantize_tile(1)
         multiply(0, 1)
+        sort_tile(2)
+        multiply(1, 0)
+        transpose_tile(2)
+        add_bias(0, 1)
+        apply_gain(0, 0, HALVES)
+        add_bias(1, 0)
+        sort_h(3, 0, VECTOR_PASSES, True)
+        sort_h(3, VECTOR_PASSES, PASSES, True)
+        round_y(0, 0, HALVES)
+        quantize_tile(2)
+        multiply(1, 1)
 
-        for i in range(1, TILES):
-            if i + 1 < TILES:
-                transpose_h(i + 1)
-            if i >= 2:
-                transpose_y(i - 2, 0, HALVES)
+        last = TILES - 1
+        for i in range(2, last):
+            transpose_tile(i + 1)
+            transpose_y(i - 2, 0, HALVES)
             add_bias(i - 1, 1)
             if i + 2 < TILES:
-                sort_h(i + 2, 0)
-                sort_h(i + 2, 1)
+                sort_tile(i + 2)
             apply_gain(i - 1, 0, HALVES)
             round_y(i - 1, 0, HALVES)
-            if i + 1 < TILES:
-                quantize_h(i + 1)
-            if i >= 2:
-                quantize_y(i - 2, 0, HALVES)
+            quantize_tile(i + 1)
+            quantize_y(i - 2, 0, HALVES)
             multiply(i, 0)
             add_bias(i, 0)
             multiply(i, 1)
 
-        last = TILES - 1
+        transpose_y(last - 2, 0, HALVES)
+        add_bias(last - 1, 1)
+        for h in range(HALVES):
+            apply_gain(last - 1, h, h + 1)
+            round_y(last - 1, h, h + 1)
+        quantize_y(last - 2, 0, HALVES)
+        multiply(last, 0)
+        add_bias(last, 0)
         apply_gain(last, 0, 1)
         round_y(last, 0, 1)
+        multiply(last, 1)
         transpose_y(last - 1, 0, HALVES)
         transpose_y(last, 0, 1)
         add_bias(last, 1)
-        quantize_y(last - 1, 0, HALVES)
-        apply_gain(last, 1, HALVES)
-        round_y(last, 1, HALVES)
-        quantize_y(last, 0, 1)
+        gain_and_round(last, 1)
         transpose_y(last, 1, HALVES)
+        apply_gain(last, 1, HALVES)
+        quantize_y(last - 1, 0, HALVES)
+        quantize_y(last, 0, 1)
         quantize_y(last, 1, HALVES)

@@ -98,33 +98,32 @@ def tile_shared_kv_latent_gain_g4_kernel(tc, hidden, w_words, w_scales, bias, ga
             for g in range(a, b):
                 sorted_h[i, g] = tile[:, :, (g - a) * P : (g - a + 1) * P]
 
-        def view_h(i, a, b):
-            words = raw[i, a][:].bitcast(F32).rearrange("m (w u) -> m u w", u=2)
-            for g in range(a, b):
-                sorted_h[i, g] = words[:, :, (g - a) * P : (g - a + 1) * P]
-
-        def transpose_h(i, a, b):
+        def transpose_h(passes):
             bank = take_bank()
-            n = b - a
-            for j in range(n):
+            n = len(passes)
+            for j, key in enumerate(passes):
                 for u in range(2):
                     col = (2 * j + u) * P
-                    nc.tensor.transpose(bank[:, col : col + P], sorted_h[i, a + j][:, u, :], ident[:])
+                    nc.tensor.transpose(bank[:, col : col + P], sorted_h[key][:, u, :], ident[:])
             tile = work.tile([P, n * GROUP], BF16, name="grouped", tag="grouped", bufs=6, align_bytes=256)
             nc.scalar.copy(
                 out=tile[:].bitcast(F32).rearrange("p (j m u) -> p j m u", j=n, u=2),
                 in_=bank[:, : 2 * n * P].rearrange("p (j u m) -> p j m u", j=n, u=2),
             )
-            grouped_h[i, a] = tile
+            grouped_h[passes] = tile
 
-        def quantize_h(i, a, b):
-            n = b - a
-            codes = work.tile([P, n * P], U32, name="hcodes", tag="hcodes", bufs=9, align_bytes=256)
-            plane = work.tile([P, n * P], U8, name="hscale", tag="hscale", bufs=9, align_bytes=256)
-            nc.vector.quantize_mx(out=codes[:].bitcast(FP8X4), scales=plane[:], in_=grouped_h[i, a][:])
-            for j in range(n):
-                h_codes[i, a + j] = codes[:, j * P : (j + 1) * P]
-                h_scales[i, a + j] = plane[:, j * P : (j + 1) * P]
+        def quantize_h(passes):
+            n = len(passes)
+            codes = work.tile([P, n * P], U32, name="hcodes", tag="hcodes", bufs=12, align_bytes=256)
+            plane = work.tile([P, n * P], U8, name="hscale", tag="hscale", bufs=12, align_bytes=256)
+            nc.vector.quantize_mx(out=codes[:].bitcast(FP8X4), scales=plane[:], in_=grouped_h[passes][:])
+            for j, key in enumerate(passes):
+                h_codes[key] = codes[:, j * P : (j + 1) * P]
+                h_scales[key] = plane[:, j * P : (j + 1) * P]
+
+        def bank_loads(tiles):
+            keys = [(i, g) for i in tiles for g in range(PASSES)]
+            return [tuple(keys[s : s + 2]) for s in range(0, len(keys), 2)]
 
         def multiply(i, h, a=0, b=PASSES):
             if a == 0:
@@ -148,13 +147,13 @@ def tile_shared_kv_latent_gain_g4_kernel(tc, hidden, w_words, w_scales, bias, ga
 
         def apply_gain(i, a, b):
             if a == 0:
-                y_f32[i] = work.tile([P, R], F32, name="y", tag="y", bufs=8)
+                y_f32[i] = work.tile([P, R], F32, name="y", tag="y", bufs=7)
             cols = slice(a * GROUP, b * GROUP)
             nc.vector.tensor_tensor(out=y_f32[i][:, cols], in0=biased[i][:, cols], in1=spread[1][:, cols], op=MULT)
             nc.sync.dma_start(out=y_rows[i * P : (i + 1) * P, cols], in_=y_f32[i][:, cols])
 
         def round_y(i, a, b):
-            tile = work.tile([P, 2, (b - a) * P, 2], BF16, name="pairs", tag="pairs")
+            tile = work.tile([P, 2, (b - a) * P, 2], BF16, name="pairs", tag="pairs", bufs=6)
             nc.scalar.copy(
                 out=tile[:], in_=y_f32[i][:, a * GROUP : b * GROUP].rearrange("m (w u e) -> m u w e", u=2, e=2)
             )
@@ -164,7 +163,7 @@ def tile_shared_kv_latent_gain_g4_kernel(tc, hidden, w_words, w_scales, bias, ga
 
         def gain_and_round(i, h):
             cols = slice(h * GROUP, (h + 1) * GROUP)
-            tile = work.tile([P, 2, P, 2], BF16, name="pairs", tag="pairs")
+            tile = work.tile([P, 2, P, 2], BF16, name="pairs", tag="pairs", bufs=6)
             nc.vector.tensor_tensor(
                 out=tile[:],
                 in0=biased[i][:, cols].rearrange("m (w u e) -> m u w e", u=2, e=2),
@@ -180,7 +179,7 @@ def tile_shared_kv_latent_gain_g4_kernel(tc, hidden, w_words, w_scales, bias, ga
                 for u in range(2):
                     col = (2 * j + u) * P
                     nc.tensor.transpose(bank[:, col : col + P], y_pairs[i, a + j][:, u, :], ident[:])
-            tile = work.tile([P, n * GROUP], BF16, name="groupedy", tag="groupedy", align_bytes=256)
+            tile = work.tile([P, n * GROUP], BF16, name="groupedy", tag="groupedy", bufs=4, align_bytes=256)
             nc.scalar.copy(
                 out=tile[:].bitcast(F32).rearrange("p (j m u) -> p j m u", j=n, u=2),
                 in_=bank[:, : 2 * n * P].rearrange("p (j u m) -> p j m u", j=n, u=2),
@@ -224,38 +223,6 @@ def tile_shared_kv_latent_gain_g4_kernel(tc, hidden, w_words, w_scales, bias, ga
                 in_=spread_bank[v][:].rearrange("m (j n) -> m n j", j=4),
             )
 
-        def finish_in_quarters(i, h):
-            pairs = work.tile([P, 2, P, 2], BF16, name="pairs", tag="pairs")
-            quarter_cols = [slice(h * GROUP + q * P, h * GROUP + (q + 1) * P) for q in range(4)]
-
-            def quarter_pairs(q):
-                nc.vector.tensor_tensor(
-                    out=pairs[:, :, q * 32 : (q + 1) * 32, :],
-                    in0=biased[i][:, quarter_cols[q]].rearrange("m (w u e) -> m u w e", u=2, e=2),
-                    in1=spread[1][:, quarter_cols[q]].rearrange("m (w u e) -> m u w e", u=2, e=2),
-                    op=MULT,
-                )
-
-            for q in range(4):
-                bank = take_bank()
-                for g in range(PASSES):
-                    nc.tensor.matmul_mx(
-                        out=bank[:, :P],
-                        lhsT=h_codes[i, g].bitcast(FP8X4),
-                        lhsT_scale=h_scales[i, g],
-                        rhs=w_tiles[h][:, g, 2 * q * P : 2 * (q + 1) * P].bitcast(FP4X4),
-                        rhs_scale=w_planes[h][:, g, q * P : (q + 1) * P],
-                        start=(g == 0),
-                        stop=(g == PASSES - 1),
-                    )
-                nc.vector.tensor_tensor(
-                    out=biased[i][:, quarter_cols[q]], in0=bank[:, :P], in1=spread[0][:, quarter_cols[q]], op=ADD
-                )
-                if q > 0:
-                    quarter_pairs(q - 1)
-            quarter_pairs(3)
-            y_pairs[i, h] = pairs[:].rearrange("m u w e -> m (u w e)").bitcast(F32).rearrange("m (u w) -> m u w", u=2)
-
         nc.scalar.dma_start(out=short[0][:], in_=bias.rearrange("(n c) -> n c", n=P))
         nc.scalar.dma_start(out=short[1][:], in_=gain.rearrange("(n c) -> n c", n=P))
         for h in range(HALVES):
@@ -280,12 +247,12 @@ def tile_shared_kv_latent_gain_g4_kernel(tc, hidden, w_words, w_scales, bias, ga
             sort_h(i, VECTOR_PASSES, PASSES, False)
 
         def transpose_tile(i):
-            for a, b in BANK_PASSES:
-                transpose_h(i, a, b)
+            for passes in bank_loads([i]):
+                transpose_h(passes)
 
         def quantize_tile(i):
-            for a, b in BANK_PASSES:
-                quantize_h(i, a, b)
+            for passes in bank_loads([i]):
+                quantize_h(passes)
 
         for a, b in BANK_PASSES:
             sort_h(0, a, b, True)
@@ -314,25 +281,62 @@ def tile_shared_kv_latent_gain_g4_kernel(tc, hidden, w_words, w_scales, bias, ga
         multiply(1, 1)
 
         last = TILES - 1
-        for i in range(2, last):
-            transpose_tile(i + 1)
-            transpose_y(i - 2, 0, HALVES)
-            add_bias(i - 1, 1)
-            if i + 2 < TILES:
-                sort_tile(i + 2)
-            apply_gain(i - 1, 0, HALVES)
-            round_y(i - 1, 0, HALVES)
-            quantize_tile(i + 1)
-            quantize_y(i - 2, 0, HALVES)
-            multiply(i, 0)
-            add_bias(i, 0)
-            multiply(i, 1)
+        turned = {0}
 
+        def pair_round(a):
+            loads = bank_loads([i for i in (a + 1, a + 2) if i < TILES])
+            late = [i for i in (a - 3, a - 2) if i not in turned and i >= 0]
+            ahead = [i for i in (a + 3, a + 4) if i < TILES]
+            for passes in loads:
+                transpose_h(passes)
+            for i in late:
+                transpose_y(i, 0, HALVES)
+                turned.add(i)
+            add_bias(a - 1, 1)
+            for i in ahead[:1]:
+                sort_tile(i)
+            apply_gain(a - 1, 0, HALVES)
+            round_y(a - 1, 0, HALVES)
+            for passes in loads:
+                quantize_h(passes)
+            multiply(a, 0)
+            add_bias(a, 0)
+            for i in late:
+                quantize_y(i, 0, HALVES)
+            multiply(a, 1)
+            apply_gain(a, 0, 1)
+            round_y(a, 0, 1)
+            add_bias(a, 1)
+            for i in ahead[1:]:
+                sort_tile(i)
+            apply_gain(a, 1, HALVES)
+            round_y(a, 1, HALVES)
+            multiply(a + 1, 0)
+            add_bias(a + 1, 0)
+            multiply(a + 1, 1)
+
+        transpose_tile(3)
+        transpose_y(0, 0, HALVES)
+        add_bias(1, 1)
+        sort_tile(4)
+        apply_gain(1, 0, HALVES)
+        round_y(1, 0, HALVES)
+        quantize_tile(3)
+        quantize_y(0, 0, HALVES)
+        multiply(2, 0)
+        add_bias(2, 0)
+        sort_tile(5)
+        multiply(2, 1)
+        for a in range(3, last, 2):
+            pair_round(a)
+
+        transpose_y(last - 3, 0, HALVES)
         transpose_y(last - 2, 0, HALVES)
         add_bias(last - 1, 1)
         for h in range(HALVES):
             apply_gain(last - 1, h, h + 1)
             round_y(last - 1, h, h + 1)
+        quantize_y(last - 3, 0, HALVES)
         quantize_y(last - 2, 0, HALVES)
         multiply(last, 0)
         add_bias(last, 0)

@@ -25,7 +25,7 @@ BANKS = 8
 VECTOR_PASSES = 3
 BANK_PASSES = ((0, 2), (2, 4), (4, 5))
 CODE_CHUNKS = ((0, 4), (4, 8), (8, 12), (12, 14), (14, 15), (15, 16))
-SCALE_CHUNKS = ((0, 13), (13, 16))
+SCALE_CHUNKS = ((0, 12), (12, 16))
 
 
 def tile_shared_kv_latent_gain_g4_kernel(tc, hidden, w_words, w_scales, bias, gain, out_0, out_1, out_2):
@@ -92,7 +92,11 @@ def tile_shared_kv_latent_gain_g4_kernel(tc, hidden, w_words, w_scales, bias, ga
             tile = work.tile([P, 2, (b - a) * P], F32, name=tag, tag=tag)
             words = raw[i, a][:].bitcast(F32).rearrange("m (w u) -> m u w", u=2)
             if on_vector:
-                nc.vector.tensor_copy(out=tile[:], in_=words)
+                n = b - a
+                nc.vector.tensor_copy(
+                    out=tile[:].rearrange("m u (g s w) -> m s g u w", g=n, s=2),
+                    in_=words.rearrange("m u (g s w) -> m s g u w", g=n, s=2),
+                )
             else:
                 nc.scalar.copy(out=tile[:], in_=words)
             for g in range(a, b):

from contextlib import ExitStack

import concourse.mybir as mybir
from concourse.masks import make_identity

TOKENS, D, R = 2048, 2560, 1024
FLOPS = 2 * TOKENS * D * R

F32 = mybir.dt.float32
BF16 = mybir.dt.bfloat16
I32 = mybir.dt.int32
U32 = mybir.dt.uint32
U8 = mybir.dt.uint8
FP8X4 = mybir.dt.float8_e4m3fn_x4
FP4X4 = mybir.dt.float4_e2m1fn_x4
ADD = mybir.AluOpType.add
MULT = mybir.AluOpType.mult

P = 128
GROUP = 512
TILES = TOKENS // P
PASSES = D // GROUP
HALVES = R // GROUP
BANKS = 8
VECTOR_PASSES = 3
BANK_PASSES = ((0, 2), (2, 4), (4, 5))
CODE_CHUNKS = ((0, 4), (4, 8), (8, 12), (12, 14), (14, 15), (15, 16))
SCALE_CHUNKS = ((0, 12), (12, 16))


def tile_shared_kv_latent_gain_g4_kernel(tc, hidden, w_words, w_scales, bias, gain, out_0, out_1, out_2):
    nc = tc.nc
    h_rows = hidden.rearrange("b s d -> (b s) d")
    y_rows = out_0.rearrange("b s r -> (b s) r")
    code_rows = out_1.rearrange("g p m t -> p g (m t)")
    w_scale_rows = w_scales.rearrange("g (q r) n -> r q g n", r=4)
    y_scale_rows = out_2.rearrange("g (q r) m -> r q g m", r=4)

    with ExitStack() as ctx:
        keep = ctx.enter_context(tc.tile_pool(name="keep", bufs=1))
        work = ctx.enter_context(tc.tile_pool(name="work", bufs=3))
        psum = ctx.enter_context(tc.psum_pool(name="psum", bufs=1))
        ctx.enter_context(tc.manual_schedule())

        banks_taken = []

        def take_bank():
            tag = "bank%d" % (len(banks_taken) % BANKS)
            banks_taken.append(tag)
            return psum.tile([P, GROUP], F32, name=tag, tag=tag)

        raw = {}
        sorted_h = {}
        grouped_h = {}
        h_codes = {}
        h_scales = {}
        acc = {}
        biased = {}
        y_f32 = {}
        y_pairs = {}
        grouped_y = {}
        spread_bank = {}

        ident = keep.tile([P, P], F32, name="ident")
        w_tiles = [keep.tile([P, PASSES, 2 * GROUP], U8, name="w%d" % h, align_bytes=256) for h in range(HALVES)]
        w_planes = [keep.tile([P, PASSES, GROUP], U8, name="wscale%d" % h, align_bytes=256) for h in range(HALVES)]
        y_codes = [keep.tile([P, HALVES, (b - a) * P], U32, name="ycodes%d" % a, align_bytes=256) for a, b in CODE_CHUNKS]
        y_planes = [keep.tile([P, HALVES, (b - a) * P], U8, name="yscale%d" % a, align_bytes=256) for a, b in SCALE_CHUNKS]
        short = [keep.tile([P, R // P], BF16, name="short%d" % v) for v in range(2)]
        spread = [keep.tile([P, R], BF16, name="spread%d" % v) for v in range(2)]

        def load_h(i, a, b):
            tile = keep.tile([P, (b - a) * GROUP], BF16, name="raw%d_%d" % (i, a))
            nc.sync.dma_start(out=tile[:], in_=h_rows[i * P : (i + 1) * P, a * GROUP : b * GROUP])
            raw[i, a] = tile

        def load_w_scales(h):
            for r in range(4):
                nc.sync.dma_start(
                    out=w_planes[h][r:P:32, :, :].bitcast(I32),
                    in_=w_scale_rows[r][:, :, h * GROUP : (h + 1) * GROUP].bitcast(I32),
                )

        def load_w(h, a, b):
            nc.sync.dma_start(
                out=w_tiles[h][:, a:b, :].bitcast(I32),
                in_=w_words[a:b, :, 2 * h * GROUP : 2 * (h + 1) * GROUP].rearrange("g p n -> p g n").bitcast(I32),
            )

        def sort_h(i, a, b, on_vector):
            tag = "sorted_v" if on_vector else "sorted_s"
            tile = work.tile([P, 2, (b - a) * P], F32, name=tag, tag=tag)
            words = raw[i, a][:].bitcast(F32).rearrange("m (w u) -> m u w", u=2)
            if on_vector:
                n = b - a
                nc.vector.tensor_copy(
                    out=tile[:].rearrange("m u (g s w) -> m s g u w", g=n, s=2),
                    in_=words.rearrange("m u (g s w) -> m s g u w", g=n, s=2),
                )
            else:
                nc.scalar.copy(out=tile[:], in_=words)
            for g in range(a, b):
                sorted_h[i, g] = tile[:, :, (g - a) * P : (g - a + 1) * P]

        def transpose_h(passes):
            bank = take_bank()
            n = len(passes)
            for j, key in enumerate(passes):
                for u in range(2):
                    col = (2 * j + u) * P
                    nc.tensor.transpose(bank[:, col : col + P], sorted_h[key][:, u, :], ident[:])
            tile = work.tile([P, n * GROUP], BF16, name="grouped", tag="grouped", bufs=6, align_bytes=256)
            nc.scalar.copy(
                out=tile[:].bitcast(F32).rearrange("p (j m u) -> p j m u", j=n, u=2),
                in_=bank[:, : 2 * n * P].rearrange("p (j u m) -> p j m u", j=n, u=2),
            )
            grouped_h[passes] = tile

        def quantize_h(passes):
            n = len(passes)
            codes = work.tile([P, n * P], U32, name="hcodes", tag="hcodes", bufs=12, align_bytes=256)
            plane = work.tile([P, n * P], U8, name="hscale", tag="hscale", bufs=12, align_bytes=256)
            nc.vector.quantize_mx(out=codes[:].bitcast(FP8X4), scales=plane[:], in_=grouped_h[passes][:])
            for j, key in enumerate(passes):
                h_codes[key] = codes[:, j * P : (j + 1) * P]
                h_scales[key] = plane[:, j * P : (j + 1) * P]

        def bank_loads(tiles):
            keys = [(i, g) for i in tiles for g in range(PASSES)]
            return [tuple(keys[s : s + 2]) for s in range(0, len(keys), 2)]

        def multiply(i, h, a=0, b=PASSES):
            if a == 0:
                acc[i, h] = take_bank()
            for g in range(a, b):
                nc.tensor.matmul_mx(
                    out=acc[i, h][:],
                    lhsT=h_codes[i, g].bitcast(FP8X4),
                    lhsT_scale=h_scales[i, g],
                    rhs=w_tiles[h][:, g, :].bitcast(FP4X4),
                    rhs_scale=w_planes[h][:, g, :],
                    start=(g == 0),
                    stop=(g == PASSES - 1),
                )

        def add_bias(i, h):
            if h == 0:
                biased[i] = work.tile([P, R], F32, name="biased", tag="biased")
            cols = slice(h * GROUP, (h + 1) * GROUP)
            nc.vector.tensor_tensor(out=biased[i][:, cols], in0=acc[i, h][:], in1=spread[0][:, cols], op=ADD)

        def apply_gain(i, a, b):
            if a == 0:
                y_f32[i] = work.tile([P, R], F32, name="y", tag="y", bufs=7)
            cols = slice(a * GROUP, b * GROUP)
            nc.vector.tensor_tensor(out=y_f32[i][:, cols], in0=biased[i][:, cols], in1=spread[1][:, cols], op=MULT)
            nc.sync.dma_start(out=y_rows[i * P : (i + 1) * P, cols], in_=y_f32[i][:, cols])

        def round_y(i, a, b):
            tile = work.tile([P, 2, (b - a) * P, 2], BF16, name="pairs", tag="pairs", bufs=6)
            nc.scalar.copy(
                out=tile[:], in_=y_f32[i][:, a * GROUP : b * GROUP].rearrange("m (w u e) -> m u w e", u=2, e=2)
            )
            words = tile[:].rearrange("m u w e -> m (u w e)").bitcast(F32).rearrange("m (u w) -> m u w", u=2)
            for h in range(a, b):
                y_pairs[i, h] = words[:, :, (h - a) * P : (h - a + 1) * P]

        def gain_and_round(i, h):
            cols = slice(h * GROUP, (h + 1) * GROUP)
            tile = work.tile([P, 2, P, 2], BF16, name="pairs", tag="pairs", bufs=6)
            nc.vector.tensor_tensor(
                out=tile[:],
                in0=biased[i][:, cols].rearrange("m (w u e) -> m u w e", u=2, e=2),
                in1=spread[1][:, cols].rearrange("m (w u e) -> m u w e", u=2, e=2),
                op=MULT,
            )
            y_pairs[i, h] = tile[:].rearrange("m u w e -> m (u w e)").bitcast(F32).rearrange("m (u w) -> m u w", u=2)

        def transpose_y(i, a, b):
            bank = take_bank()
            n = b - a
            for j in range(n):
                for u in range(2):
                    col = (2 * j + u) * P
                    nc.tensor.transpose(bank[:, col : col + P], y_pairs[i, a + j][:, u, :], ident[:])
            tile = work.tile([P, n * GROUP], BF16, name="groupedy", tag="groupedy", bufs=4, align_bytes=256)
            nc.scalar.copy(
                out=tile[:].bitcast(F32).rearrange("p (j m u) -> p j m u", j=n, u=2),
                in_=bank[:, : 2 * n * P].rearrange("p (j u m) -> p j m u", j=n, u=2),
            )
            for j in range(n):
                grouped_y[i, a + j] = tile[:, j * GROUP : (j + 1) * GROUP]

        def quantize_y(i, a, b):
            cc = [c for c, (lo, hi) in enumerate(CODE_CHUNKS) if lo <= i < hi][0]
            sc = [c for c, (lo, hi) in enumerate(SCALE_CHUNKS) if lo <= i < hi][0]
            c0 = (i - CODE_CHUNKS[cc][0]) * P
            s0 = (i - SCALE_CHUNKS[sc][0]) * P
            for h in range(a, b):
                nc.vector.quantize_mx(
                    out=y_codes[cc][:, h, c0 : c0 + P].bitcast(FP8X4),
                    scales=y_planes[sc][:, h, s0 : s0 + P],
                    in_=grouped_y[i, h],
                )
            if b == HALVES and i + 1 == CODE_CHUNKS[cc][1]:
                lo, hi = CODE_CHUNKS[cc]
                nc.sync.dma_start(out=code_rows[:, :, 4 * lo * P : 4 * hi * P].bitcast(I32), in_=y_codes[cc][:].bitcast(I32))
            if b == HALVES and i + 1 == SCALE_CHUNKS[sc][1]:
                lo, hi = SCALE_CHUNKS[sc]
                for r in range(4):
                    queue = nc.sync if r % 2 == 0 or hi < TILES else nc.scalar
                    queue.dma_start(
                        out=y_scale_rows[r][:, :, lo * P : hi * P].bitcast(I32), in_=y_planes[sc][r:P:32, :, :].bitcast(I32)
                    )

        def spread_transpose(v):
            spread_bank[v] = take_bank()
            words = short[v][:].bitcast(F32)
            for j in range(4):
                nc.tensor.transpose(
                    spread_bank[v][:, j * P : (j + 1) * P], words[:, j : j + 1].to_broadcast([P, P]), ident[:]
                )

        def spread_copy(v):
            nc.scalar.copy(
                out=spread[v][:].bitcast(F32).rearrange("m (n j) -> m n j", j=4),
                in_=spread_bank[v][:].rearrange("m (j n) -> m n j", j=4),
            )

        nc.scalar.dma_start(out=short[0][:], in_=bias.rearrange("(n c) -> n c", n=P))
        nc.scalar.dma_start(out=short[1][:], in_=gain.rearrange("(n c) -> n c", n=P))
        for h in range(HALVES):
            nc.vector.memset(w_planes[h][:].bitcast(I32), 0)
        make_identity(nc, ident[:])
        for a, b in BANK_PASSES:
            load_h(0, a, b)
        load_w_scales(0)
        load_w(0, 0, 2)
        load_w(0, 2, PASSES)
        load_h(1, 0, VECTOR_PASSES)
        load_h(1, VECTOR_PASSES, PASSES)
        load_w_scales(1)
        load_w(1, 0, 2)
        load_w(1, 2, PASSES)
        for i in range(2, TILES):
            load_h(i, 0, VECTOR_PASSES)
            load_h(i, VECTOR_PASSES, PASSES)

        def sort_tile(i):
            sort_h(i, 0, VECTOR_PASSES, True)
            sort_h(i, VECTOR_PASSES, PASSES, False)

        def transpose_tile(i):
            for passes in bank_loads([i]):
                transpose_h(passes)

        def quantize_tile(i):
            for passes in bank_loads([i]):
                quantize_h(passes)

        for a, b in BANK_PASSES:
            sort_h(0, a, b, True)
        spread_transpose(0)
        transpose_tile(0)
        spread_transpose(1)
        spread_copy(0)
        spread_copy(1)
        quantize_tile(0)
        sort_tile(1)
        multiply(0, 0)
        transpose_tile(1)
        add_bias(0, 0)
        quantize_tile(1)
        multiply(0, 1)
        sort_tile(2)
        multiply(1, 0)
        transpose_tile(2)
        add_bias(0, 1)
        apply_gain(0, 0, HALVES)
        add_bias(1, 0)
        sort_h(3, 0, VECTOR_PASSES, True)
        sort_h(3, VECTOR_PASSES, PASSES, True)
        round_y(0, 0, HALVES)
        quantize_tile(2)
        multiply(1, 1)

        last = TILES - 1
        turned = {0}

        def pair_round(a):
            loads = bank_loads([i for i in (a + 1, a + 2) if i < TILES])
            late = [i for i in (a - 3, a - 2) if i not in turned and i >= 0]
            ahead = [i for i in (a + 3, a + 4) if i < TILES]
            for passes in loads:
                transpose_h(passes)
            for i in late:
                transpose_y(i, 0, HALVES)
                turned.add(i)
            add_bias(a - 1, 1)
            for i in ahead[:1]:
                sort_tile(i)
            apply_gain(a - 1, 0, HALVES)
            round_y(a - 1, 0, HALVES)
            for passes in loads:
                quantize_h(passes)
            multiply(a, 0)
            add_bias(a, 0)
            for i in late:
                quantize_y(i, 0, HALVES)
            multiply(a, 1)
            apply_gain(a, 0, 1)
            round_y(a, 0, 1)
            add_bias(a, 1)
            for i in ahead[1:]:
                sort_tile(i)
            apply_gain(a, 1, HALVES)
            round_y(a, 1, HALVES)
            multiply(a + 1, 0)
            add_bias(a + 1, 0)
            multiply(a + 1, 1)

        transpose_tile(3)
        transpose_y(0, 0, HALVES)
        add_bias(1, 1)
        sort_tile(4)
        apply_gain(1, 0, HALVES)
        round_y(1, 0, HALVES)
        quantize_tile(3)
        quantize_y(0, 0, HALVES)
        multiply(2, 0)
        add_bias(2, 0)
        sort_tile(5)
        multiply(2, 1)
        for a in range(3, last, 2):
            pair_round(a)

        transpose_y(last - 3, 0, HALVES)
        transpose_y(last - 2, 0, HALVES)
        add_bias(last - 1, 1)
        for h in range(HALVES):
            apply_gain(last - 1, h, h + 1)
            round_y(last - 1, h, h + 1)
        quantize_y(last - 3, 0, HALVES)
        quantize_y(last - 2, 0, HALVES)
        multiply(last, 0)
        add_bias(last, 0)
        apply_gain(last, 0, 1)
        round_y(last, 0, 1)
        multiply(last, 1)
        transpose_y(last - 1, 0, HALVES)
        transpose_y(last, 0, 1)
        add_bias(last, 1)
        gain_and_round(last, 1)
        transpose_y(last, 1, HALVES)
        apply_gain(last, 1, HALVES)
        quantize_y(last - 1, 0, HALVES)
        quantize_y(last, 0, 1)
        quantize_y(last, 1, HALVES)
